import numpy as np
import ml_dtypes


def mxq(x, axis, fmt="e4m3"):
    dtype, down = {"e4m3": (ml_dtypes.float8_e4m3fn, 7), "e5m2": (ml_dtypes.float8_e5m2, 14)}[fmt]
    v = np.moveaxis(np.asarray(x, np.float32).astype(ml_dtypes.bfloat16).astype(np.float64), axis, -1)
    blocks = v.reshape(v.shape[:-1] + (-1, 32))
    amax = np.abs(blocks).max(-1, keepdims=True)
    byte = np.maximum(np.where(amax > 0, np.frexp(amax)[1] - 1 + 127, 0) - down, 1)
    scale = np.exp2(byte - 127.0)
    codes = (blocks / scale).astype(np.float32).astype(dtype).astype(np.float64)
    return np.moveaxis((codes * scale).reshape(v.shape), -1, axis)


WIDE = False


def mx_kscale(k):
    if not WIDE:
        return np.ones(k)
    levels = np.array([30, -30])
    if k % 512:
        return np.exp2(np.random.permutation(np.resize(levels, k // 32))).repeat(32)
    a = np.empty((k // 512, 16))
    for p in range(k // 512):
        a[p, :8] = np.random.permutation(np.resize(levels, 8))
        for g in range(8):
            far = levels[np.abs(levels - a[p, g]) >= 10]
            a[p, g + 8] = far[np.random.randint(len(far))]
    return np.exp2(a.ravel()).repeat(32)


def f64(x):
    return np.asarray(x).astype(np.float64)


def striped(idx):
    return np.tile(np.asarray(idx).reshape(-1, 16).T, (8, 1)).astype(np.uint16)


def unstriped(offs):
    return offs[:16].T.reshape(-1).astype(np.int64)


E2M1 = np.array([0.0, 0.5, 1.0, 1.5, 2.0, 3.0, 4.0, 6.0, -0.0, -0.5, -1.0, -1.5, -2.0, -3.0, -4.0, -6.0])


def pack_weight(w, fmt):
    k, n = w.shape
    w = f64(np.asarray(w, np.float32).astype(ml_dtypes.bfloat16)).reshape(k // 32, 32, n)
    amax = np.abs(w).max(1)
    if fmt in ("e4m3", "e5m2"):
        byte = np.frexp(amax)[1] - 1 + 127 - (7 if fmt == "e4m3" else 14)
    else:
        mant, ex = np.frexp(amax / 6.0)
        byte = np.where(mant > 0.5, ex, ex - 1) + 127
    byte = np.clip(np.where(amax > 0, byte, 1), 1, 254)
    scaled = (w * np.exp2(127.0 - byte)[:, None, :]).reshape(k, n).astype(np.float32)
    by_word = np.ascontiguousarray(scaled.reshape(k // 512, 128, 4, n).transpose(0, 1, 3, 2))
    if fmt in ("e4m3", "e5m2"):
        words = by_word.astype(ml_dtypes.float8_e4m3fn if fmt == "e4m3" else ml_dtypes.float8_e5m2).view(np.uint8)
    else:
        c = by_word.astype(ml_dtypes.float4_e2m1fn).view(np.uint8) & 0xF
        words = (c[..., 0::2] | (c[..., 1::2] << 4)).reshape(k // 512, 128, 2 * n)
    return np.ascontiguousarray(words), np.ascontiguousarray(byte.astype(np.uint8).reshape(k // 512, 16, n))


def unpack_weight(words, scales, fmt):
    g, _, n = scales.shape
    words = np.ascontiguousarray(words).reshape(g, 128, n, -1)
    if fmt in ("e4m3", "e5m2"):
        vals = words.view(ml_dtypes.float8_e4m3fn if fmt == "e4m3" else ml_dtypes.float8_e5m2).astype(np.float64)
    else:
        nib = np.empty((g, 128, n, 4), np.uint8)
        nib[..., 0::2] = words & 0xF
        nib[..., 1::2] = words >> 4
        vals = E2M1[nib]
    vals = vals * np.repeat(np.exp2(scales.astype(np.float64) - 127.0), 8, axis=1)[..., None]
    return vals.transpose(0, 1, 3, 2).reshape(g * 512, n)


K, T, J, I, R, C, S = 512, 512, 256, 256, 512, 512, 64


def setup_inputs():
    n = np.random.standard_normal
    idx = np.random.permutation(T)[:J]
    idx2 = np.random.permutation(T)[:I]
    idx3 = np.random.permutation(C)[:I]
    fk = mx_kscale(K)
    fr = mx_kscale(R)
    xtp = pack_weight(n((K, T)) / fk[:, None], "e5m2")
    wap = pack_weight(n((K, R)) * 0.5 / np.sqrt(K) * fk[:, None] * fr, "e4m3")
    wbp = pack_weight(n((K, R)) * 1 / np.sqrt(K) * fk[:, None] / fr, "e2m1")
    return {
        "xt_words": xtp[0],
        "xt_scales": xtp[1],
        "wa_words": wap[0],
        "wa_scales": wap[1],
        "wb_words": wbp[0],
        "wb_scales": wbp[1],
        "tf": (n((R, C))).astype(np.float32),
        "cw1": (np.random.uniform(-1.0, 1.0, (1, I))).astype(np.float32),
        "offs": striped(idx),
        "offs2": striped(idx2),
        "offs3": striped(idx3),
    }


def reference(xt_words, xt_scales, wa_words, wa_scales, wb_words, wb_scales, tf, cw1, offs, offs2, offs3):
    idx = unstriped(offs)
    idx2 = unstriped(offs2)
    idx3 = unstriped(offs3)
    xtu = unpack_weight(xt_words, xt_scales, "e5m2")
    wau = unpack_weight(wa_words, wa_scales, "e4m3")
    wbu = unpack_weight(wb_words, wb_scales, "e2m1")
    xtidxg = xtu[:, idx]
    za = wau.T @ xtidxg
    ha = np.maximum(za, 0.0)
    xtidx2g = xtu[:, idx2]
    zb = wbu.T @ xtidx2g
    hb = zb * f64(tf)[:, idx3]
    haq = mxq(ha, 0, "e5m2")
    hbq = mxq(hb, 0, "e4m3")
    a0 = haq.T @ hbq
    y = 0.04 * (a0 * f64(cw1)).reshape(J, S, I // S).sum(axis=2)
    return y

@@ -1,0 +1,179 @@
+from contextlib import ExitStack
+
+import concourse.mybir as mybir
+
+K, T, J, I, R, C, S = 512, 512, 256, 256, 512, 512, 64
+FLOPS = 2 * K * R * J + 2 * K * R * I + 2 * R * J * I
+
+F32 = mybir.dt.float32
+BF16 = mybir.dt.bfloat16
+I32 = mybir.dt.int32
+U32 = mybir.dt.uint32
+U16 = mybir.dt.uint16
+U8 = mybir.dt.uint8
+E4M3 = mybir.dt.float8_e4m3fn_x4
+E5M2 = mybir.dt.float8_e5m2_x4
+E2M1 = mybir.dt.float4_e2m1fn_x4
+MULT = mybir.AluOpType.mult
+ADD = mybir.AluOpType.add
+ACT = mybir.ActivationFunctionType
+
+P = 128
+PACK = 4
+RUN = 8
+HALF = 128
+OUT_SCALE = 0.04
+
+
+def tile_list_meet_plain_timestable_summed_kernel(
+    tc, xt_words, xt_scales, wa_words, wa_scales, wb_words, wb_scales, tf, cw1, offs, offs2, offs3, out
+):
+    nc = tc.nc
+    with ExitStack() as ctx:
+        sb = ctx.enter_context(tc.tile_pool(name="sb", bufs=1))
+        ps = ctx.enter_context(tc.psum_pool(name="ps", bufs=1))
+
+        list_a = sb.tile([P, J // 16], U16, name="list_a")
+        list_b = sb.tile([P, I // 16], U16, name="list_b")
+        list_f = sb.tile([P, I // 16], U16, name="list_f")
+        x_words = sb.tile([P, T], I32, name="x_words", align_bytes=64)
+        x_scales = sb.tile([P, T], U8, name="x_scales", align_bytes=64)
+        wa_raw = sb.tile([P, R], I32, name="wa_raw", align_bytes=64)
+        wa_raw_scales = sb.tile([P, R], U8, name="wa_raw_scales", align_bytes=64)
+        wb_raw = sb.tile([P, R // 2], I32, name="wb_raw", align_bytes=64)
+        wb_raw_scales = sb.tile([P, R], U8, name="wb_raw_scales", align_bytes=64)
+        tf_rows = [sb.tile([P, C], F32, name="tf_rows%d" % t, align_bytes=64) for t in range(PACK)]
+        cw = sb.tile([P, I], F32, name="cw", align_bytes=64)
+
+        tf_dealt = tf.rearrange("(b t q) c -> t b q c", t=PACK, q=RUN)
+
+        def load_scale_rows(queue, plane, rows, q):
+            quad = rows[0, 4 * q : 4 * q + 4, :].bitcast(I32)
+            queue.dma_start(
+                out=plane[32 * q : 32 * q + 32, :].bitcast(I32),
+                in_=quad.unsqueeze(0).to_broadcast([8, 4, R // 4]),
+            )
+
+        nc.sync.dma_start(out=list_b[:], in_=offs2)
+        nc.scalar.dma_start(out=x_words[:], in_=xt_words[0].rearrange("p n t -> p (n t)").bitcast(I32))
+        load_scale_rows(nc.sync, x_scales, xt_scales, 0)
+        load_scale_rows(nc.scalar, x_scales, xt_scales, 1)
+        load_scale_rows(nc.sync, x_scales, xt_scales, 2)
+        load_scale_rows(nc.scalar, x_scales, xt_scales, 3)
+        nc.sync.dma_start(out=list_a[:], in_=offs)
+        nc.scalar.dma_start(out=tf_rows[0][:], in_=tf_dealt[0])
+        nc.sync.dma_start(out=list_f[:], in_=offs3)
+        nc.sync.dma_start(out=wb_raw[:], in_=wb_words[0].bitcast(I32))
+        load_scale_rows(nc.sync, wb_raw_scales, wb_scales, 0)
+        load_scale_rows(nc.sync, wb_raw_scales, wb_scales, 1)
+        load_scale_rows(nc.sync, wb_raw_scales, wb_scales, 2)
+        load_scale_rows(nc.sync, wb_raw_scales, wb_scales, 3)
+        nc.sync.dma_start(out=tf_rows[1][:], in_=tf_dealt[1])
+        nc.sync.dma_start(out=tf_rows[2][:], in_=tf_dealt[2])
+        nc.sync.dma_start(out=tf_rows[3][:], in_=tf_dealt[3])
+        nc.sync.dma_start(out=wa_raw[:], in_=wa_words[0].rearrange("p n t -> p (n t)").bitcast(I32))
+        load_scale_rows(nc.sync, wa_raw_scales, wa_scales, 0)
+        load_scale_rows(nc.sync, wa_raw_scales, wa_scales, 1)
+        load_scale_rows(nc.sync, wa_raw_scales, wa_scales, 2)
+        load_scale_rows(nc.sync, wa_raw_scales, wa_scales, 3)
+        nc.sync.dma_start(out=cw[:], in_=cw1[0].partition_broadcast(P))
+
+        def gather_tokens(name, offsets):
+            words = sb.tile([P, J], U32, name=name + "_words", align_bytes=64)
+            scales = sb.tile([P, J], U8, name=name + "_scales", align_bytes=64)
+            nc.vector.tensor_copy(out=words[:], in_=x_words[:].bitcast(U32).indirect(offsets[:]))
+            nc.vector.tensor_copy(out=scales[:], in_=x_scales[:].indirect(offsets[:]))
+            return words, scales
+
+        def deal(name, raw):
+            width = raw.shape[1]
+            dealt = sb.tile([P, width], I32, name=name, align_bytes=64)
+            nc.vector.tensor_copy(
+                out=dealt[:].rearrange("p (t b w) -> p t b w", t=PACK, b=R // 32),
+                in_=raw.rearrange("p (b t w) -> p t b w", t=PACK, b=R // 32),
+            )
+            return dealt[:].bitcast(U8)
+
+        def first_product(name, w_bytes, w_format, w_scales, words, scales):
+            banks = []
+            width = w_bytes.shape[1] // PACK
+            for h in range(2):
+                bank = ps.tile([P, PACK, HALF], F32, name="%s%d" % (name, h))
+                cols = slice(HALF * h, HALF * (h + 1))
+                for t in range(PACK):
+                    nc.tensor.matmul_mx(
+                        out=bank[:, t, :],
+                        lhsT=w_bytes[:, width * t : width * (t + 1)].bitcast(w_format),
+                        lhsT_scale=w_scales[:, P * t : P * (t + 1)],
+                        rhs=words[:, cols].bitcast(E5M2),
+                        rhs_scale=scales[:, cols],
+                        start=True,
+                        stop=True,
+                    )
+                banks.append(bank)
+            return banks
+
+        tf_picked = sb.tile([P, PACK, I], F32, name="tf_picked", align_bytes=64)
+        for t in range(PACK):
+            nc.scalar.activation(out=tf_picked[:, t, :], in_=tf_rows[t][:].indirect(list_f[:]), func=ACT.Copy)
+
+        xb_words, xb_scales = gather_tokens("xb", list_b)
+        wb_dealt = deal("wb_dealt", wb_raw[:])
+        wb_dealt_scales = deal("wb_dealt_scales", wb_raw_scales[:].bitcast(I32))
+        zb = first_product("zb", wb_dealt, E2M1, wb_dealt_scales, xb_words, xb_scales)
+
+        xa_words, xa_scales = gather_tokens("xa", list_a)
+        wa_dealt = deal("wa_dealt", wa_raw[:])
+        wa_dealt_scales = deal("wa_dealt_scales", wa_raw_scales[:].bitcast(I32))
+        za = first_product("za", wa_dealt, E4M3, wa_dealt_scales, xa_words, xa_scales)
+
+        hb = sb.tile([P, I, PACK], BF16, name="hb", align_bytes=64)
+        for h in range(2):
+            cols = slice(HALF * h, HALF * (h + 1))
+            nc.vector.tensor_tensor(
+                out=hb[:, cols, :],
+                in0=zb[h][:].rearrange("p t n -> p n t"),
+                in1=tf_picked[:, :, cols].rearrange("p t n -> p n t"),
+                op=MULT,
+            )
+        hb_words = sb.tile([P, I], U32, name="hb_words", align_bytes=64)
+        hb_scales = sb.tile([P, I], U8, name="hb_scales", align_bytes=64)
+        nc.vector.quantize_mx(
+            out=hb_words[:].bitcast(E4M3), scales=hb_scales[:], in_=hb[:].rearrange("p n t -> p (n t)")
+        )
+
+        weighted = []
+        for h in range(2):
+            ha = sb.tile([P, HALF, PACK], BF16, name="ha%d" % h, align_bytes=64)
+            nc.scalar.activation(out=ha[:], in_=za[h][:].rearrange("p t n -> p n t"), func=ACT.Relu)
+            ha_words = sb.tile([P, HALF], U32, name="ha_words%d" % h, align_bytes=64)
+            ha_scales = sb.tile([P, HALF], U8, name="ha_scales%d" % h, align_bytes=64)
+            nc.vector.quantize_mx(
+                out=ha_words[:].bitcast(E5M2), scales=ha_scales[:], in_=ha[:].rearrange("p n t -> p (n t)")
+            )
+            scores = ps.tile([P, I], F32, name="scores%d" % h)
+            nc.tensor.matmul_mx(
+                out=scores[:],
+                lhsT=ha_words[:].bitcast(E5M2),
+                lhsT_scale=ha_scales[:],
+                rhs=hb_words[:].bitcast(E4M3),
+                rhs_scale=hb_scales[:],
+                start=True,
+                stop=True,
+            )
+            product = sb.tile([P, S, I // S], F32, name="weighted%d" % h, align_bytes=64)
+            weighted.append((scores, product))
+
+        for scores, product in weighted:
+            nc.vector.scalar_tensor_tensor(
+                out=product[:].rearrange("p s u -> p (s u)"),
+                in0=scores[:],
+                scalar=OUT_SCALE,
+                in1=cw[:],
+                op0=MULT,
+                op1=MULT,
+            )
+        for h, (scores, product) in enumerate(weighted):
+            summed = sb.tile([P, S], F32, name="summed%d" % h, align_bytes=64)
+            nc.vector.tensor_reduce(out=summed[:], in_=product[:], axis=mybir.AxisListType.X, op=ADD)
+            (nc.sync, nc.scalar)[h].dma_start(out=out[HALF * h : HALF * (h + 1), :], in_=summed[:])

@@ -20,7 +20,6 @@ ACT = mybir.ActivationFunctionType
 
 P = 128
 PACK = 4
-RUN = 8
 HALF = 128
 OUT_SCALE = 0.04
 
@@ -39,44 +38,48 @@ def tile_list_meet_plain_timestable_summed_kernel(
         x_words = sb.tile([P, T], I32, name="x_words", align_bytes=64)
         x_scales = sb.tile([P, T], U8, name="x_scales", align_bytes=64)
         wa_raw = sb.tile([P, R], I32, name="wa_raw", align_bytes=64)
-        wa_raw_scales = sb.tile([P, R], U8, name="wa_raw_scales", align_bytes=64)
-        wb_raw = sb.tile([P, R // 2], I32, name="wb_raw", align_bytes=64)
+        wa_raw_scales = sb.tile([P, R], U8, name="wa_raw_scales", tag="wa_scales_then_hb", align_bytes=64)
+        wb_raw = sb.tile([P, R], U16, name="wb_raw", align_bytes=64)
         wb_raw_scales = sb.tile([P, R], U8, name="wb_raw_scales", align_bytes=64)
-        tf_rows = [sb.tile([P, C], F32, name="tf_rows%d" % t, align_bytes=64) for t in range(PACK)]
-        cw = sb.tile([P, I], F32, name="cw", align_bytes=64)
+        tf_rows = sb.tile([P, PACK * C], F32, name="tf_rows", tag="tf_then_ha", align_bytes=64)
+        cw_runs = sb.tile([P, 8], F32, name="cw_runs", align_bytes=64)
 
-        tf_dealt = tf.rearrange("(b t q) c -> t b q c", t=PACK, q=RUN)
+        for plane in (wb_raw_scales, wa_raw_scales):
+            nc.vector.memset(plane[:].bitcast(I32), 0)
 
         def load_scale_rows(queue, plane, rows, q):
+            queue.dma_start(
+                out=plane[32 * q : 32 * q + 4, :].bitcast(I32),
+                in_=rows[0, 4 * q : 4 * q + 4, :].bitcast(I32),
+            )
+
+        def fill_scale_quadrant(queue, plane, rows, q):
             quad = rows[0, 4 * q : 4 * q + 4, :].bitcast(I32)
             queue.dma_start(
                 out=plane[32 * q : 32 * q + 32, :].bitcast(I32),
-                in_=quad.unsqueeze(0).to_broadcast([8, 4, R // 4]),
+                in_=quad.unsqueeze(0).to_broadcast([8, 4, T // 4]),
             )
 
         nc.sync.dma_start(out=list_b[:], in_=offs2)
         nc.scalar.dma_start(out=x_words[:], in_=xt_words[0].rearrange("p n t -> p (n t)").bitcast(I32))
-        load_scale_rows(nc.sync, x_scales, xt_scales, 0)
-        load_scale_rows(nc.scalar, x_scales, xt_scales, 1)
-        load_scale_rows(nc.sync, x_scales, xt_scales, 2)
-        load_scale_rows(nc.scalar, x_scales, xt_scales, 3)
+        nc.gpsimd.dma_start(out=tf_rows[:], in_=tf.rearrange("(p t) c -> p (t c)", t=PACK))
+        fill_scale_quadrant(nc.sync, x_scales, xt_scales, 0)
+        fill_scale_quadrant(nc.scalar, x_scales, xt_scales, 1)
+        fill_scale_quadrant(nc.sync, x_scales, xt_scales, 2)
+        fill_scale_quadrant(nc.scalar, x_scales, xt_scales, 3)
+        nc.sync.dma_start(out=cw_runs[:], in_=cw1[0].rearrange("(n e) -> n e", e=8).unsqueeze(0).to_broadcast([4, 32, 8]))
         nc.sync.dma_start(out=list_a[:], in_=offs)
-        nc.scalar.dma_start(out=tf_rows[0][:], in_=tf_dealt[0])
         nc.sync.dma_start(out=list_f[:], in_=offs3)
-        nc.sync.dma_start(out=wb_raw[:], in_=wb_words[0].bitcast(I32))
+        nc.sync.dma_start(out=wb_raw[:].bitcast(I32), in_=wb_words[0].bitcast(I32))
         load_scale_rows(nc.sync, wb_raw_scales, wb_scales, 0)
         load_scale_rows(nc.sync, wb_raw_scales, wb_scales, 1)
         load_scale_rows(nc.sync, wb_raw_scales, wb_scales, 2)
         load_scale_rows(nc.sync, wb_raw_scales, wb_scales, 3)
-        nc.sync.dma_start(out=tf_rows[1][:], in_=tf_dealt[1])
-        nc.sync.dma_start(out=tf_rows[2][:], in_=tf_dealt[2])
-        nc.sync.dma_start(out=tf_rows[3][:], in_=tf_dealt[3])
         nc.sync.dma_start(out=wa_raw[:], in_=wa_words[0].rearrange("p n t -> p (n t)").bitcast(I32))
         load_scale_rows(nc.sync, wa_raw_scales, wa_scales, 0)
-        load_scale_rows(nc.sync, wa_raw_scales, wa_scales, 1)
-        load_scale_rows(nc.sync, wa_raw_scales, wa_scales, 2)
-        load_scale_rows(nc.sync, wa_raw_scales, wa_scales, 3)
-        nc.sync.dma_start(out=cw[:], in_=cw1[0].partition_broadcast(P))
+        load_scale_rows(nc.gpsimd, wa_raw_scales, wa_scales, 1)
+        load_scale_rows(nc.gpsimd, wa_raw_scales, wa_scales, 2)
+        load_scale_rows(nc.gpsimd, wa_raw_scales, wa_scales, 3)
 
         def gather_tokens(name, offsets):
             words = sb.tile([P, J], U32, name=name + "_words", align_bytes=64)
@@ -85,26 +88,25 @@ def tile_list_meet_plain_timestable_summed_kernel(
             nc.vector.tensor_copy(out=scales[:], in_=x_scales[:].indirect(offsets[:]))
             return words, scales
 
-        def deal(name, raw):
-            width = raw.shape[1]
-            dealt = sb.tile([P, width], I32, name=name, align_bytes=64)
+        def deal(name, raw, dtype, line):
+            dealt = sb.tile([P, R], dtype, name=name, align_bytes=64)
             nc.vector.tensor_copy(
-                out=dealt[:].rearrange("p (t b w) -> p t b w", t=PACK, b=R // 32),
-                in_=raw.rearrange("p (b t w) -> p t b w", t=PACK, b=R // 32),
+                out=dealt[:].rearrange("p (t c i) -> p c t i", t=PACK, i=line),
+                in_=raw[:].rearrange("p (c i t) -> p c t i", t=PACK, i=line),
             )
-            return dealt[:].bitcast(U8)
+            return dealt
 
-        def first_product(name, w_bytes, w_format, w_scales, words, scales):
+        def first_product(name, w_words, w_format, w_scales, words, scales):
             banks = []
-            width = w_bytes.shape[1] // PACK
             for h in range(2):
                 bank = ps.tile([P, PACK, HALF], F32, name="%s%d" % (name, h))
                 cols = slice(HALF * h, HALF * (h + 1))
                 for t in range(PACK):
+                    rows = slice(P * t, P * (t + 1))
                     nc.tensor.matmul_mx(
                         out=bank[:, t, :],
-                        lhsT=w_bytes[:, width * t : width * (t + 1)].bitcast(w_format),
-                        lhsT_scale=w_scales[:, P * t : P * (t + 1)],
+                        lhsT=w_words[:, rows].bitcast(w_format),
+                        lhsT_scale=w_scales[:, rows],
                         rhs=words[:, cols].bitcast(E5M2),
                         rhs_scale=scales[:, cols],
                         start=True,
@@ -113,21 +115,32 @@ def tile_list_meet_plain_timestable_summed_kernel(
                 banks.append(bank)
             return banks
 
+        cw_wide = sb.tile([P, 8, 32], F32, name="cw_wide", align_bytes=64)
+        nc.scalar.activation(out=cw_wide[:], in_=cw_runs[:].unsqueeze(2).to_broadcast([P, 8, 32]), func=ACT.Copy)
+        cw_turned = sb.tile([P, 8, 32], F32, name="cw_turned", align_bytes=64)
+        nc.vector.transpose(
+            out=cw_turned[:].rearrange("p e n -> p (e n)"), in_=cw_wide[:].rearrange("p e n -> p (e n)")
+        )
+        cw = sb.tile([P, 32, 8], F32, name="cw", align_bytes=64)
+        nc.scalar.activation(out=cw[:], in_=cw_turned[:].rearrange("p e n -> p n e"), func=ACT.Copy)
+
         tf_picked = sb.tile([P, PACK, I], F32, name="tf_picked", align_bytes=64)
         for t in range(PACK):
-            nc.scalar.activation(out=tf_picked[:, t, :], in_=tf_rows[t][:].indirect(list_f[:]), func=ACT.Copy)
+            nc.scalar.activation(
+                out=tf_picked[:, t, :], in_=tf_rows[:, C * t : C * (t + 1)].indirect(list_f[:]), func=ACT.Copy
+            )
 
         xb_words, xb_scales = gather_tokens("xb", list_b)
-        wb_dealt = deal("wb_dealt", wb_raw[:])
-        wb_dealt_scales = deal("wb_dealt_scales", wb_raw_scales[:].bitcast(I32))
+        xa_words, xa_scales = gather_tokens("xa", list_a)
+        wb_dealt = deal("wb_dealt", wb_raw, U16, 8)
+        wb_dealt_scales = deal("wb_dealt_scales", wb_raw_scales, U8, 16)
         zb = first_product("zb", wb_dealt, E2M1, wb_dealt_scales, xb_words, xb_scales)
 
-        xa_words, xa_scales = gather_tokens("xa", list_a)
-        wa_dealt = deal("wa_dealt", wa_raw[:])
-        wa_dealt_scales = deal("wa_dealt_scales", wa_raw_scales[:].bitcast(I32))
+        wa_dealt = deal("wa_dealt", wa_raw, I32, 4)
+        wa_dealt_scales = deal("wa_dealt_scales", wa_raw_scales, U8, 16)
         za = first_product("za", wa_dealt, E4M3, wa_dealt_scales, xa_words, xa_scales)
 
-        hb = sb.tile([P, I, PACK], BF16, name="hb", align_bytes=64)
+        hb = sb.tile([P, I, PACK], BF16, name="hb", tag="wa_scales_then_hb", align_bytes=64)
         for h in range(2):
             cols = slice(HALF * h, HALF * (h + 1))
             nc.vector.tensor_tensor(
@@ -142,15 +155,18 @@ def tile_list_meet_plain_timestable_summed_kernel(
             out=hb_words[:].bitcast(E4M3), scales=hb_scales[:], in_=hb[:].rearrange("p n t -> p (n t)")
         )
 
+        ha = sb.tile([P, J * PACK], BF16, name="ha", tag="tf_then_ha", align_bytes=64)
         weighted = []
         for h in range(2):
-            ha = sb.tile([P, HALF, PACK], BF16, name="ha%d" % h, align_bytes=64)
-            nc.scalar.activation(out=ha[:], in_=za[h][:].rearrange("p t n -> p n t"), func=ACT.Relu)
+            ha_half = ha[:, HALF * PACK * h : HALF * PACK * (h + 1)]
+            nc.scalar.activation(
+                out=ha_half.rearrange("p (n t) -> p n t", t=PACK),
+                in_=za[h][:].rearrange("p t n -> p n t"),
+                func=ACT.Relu,
+            )
             ha_words = sb.tile([P, HALF], U32, name="ha_words%d" % h, align_bytes=64)
             ha_scales = sb.tile([P, HALF], U8, name="ha_scales%d" % h, align_bytes=64)
-            nc.vector.quantize_mx(
-                out=ha_words[:].bitcast(E5M2), scales=ha_scales[:], in_=ha[:].rearrange("p n t -> p (n t)")
-            )
+            nc.vector.quantize_mx(out=ha_words[:].bitcast(E5M2), scales=ha_scales[:], in_=ha_half)
             scores = ps.tile([P, I], F32, name="scores%d" % h)
             nc.tensor.matmul_mx(
                 out=scores[:],
@@ -169,7 +185,7 @@ def tile_list_meet_plain_timestable_summed_kernel(
                 out=product[:].rearrange("p s u -> p (s u)"),
                 in0=scores[:],
                 scalar=OUT_SCALE,
-                in1=cw[:],
+                in1=cw[:].rearrange("p n e -> p (n e)"),
                 op0=MULT,
                 op1=MULT,
             )

@@ -22,6 +22,8 @@ P = 128
 PACK = 4
 HALF = 128
 OUT_SCALE = 0.04
+TF_AT = 0
+WA_AT = 4 * PACK * C
 
 
 def tile_list_meet_plain_timestable_summed_kernel(
@@ -30,6 +32,7 @@ def tile_list_meet_plain_timestable_summed_kernel(
     nc = tc.nc
     with ExitStack() as ctx:
         sb = ctx.enter_context(tc.tile_pool(name="sb", bufs=1))
+        reused = ctx.enter_context(tc.tile_pool(name="reused", bufs=1))
         ps = ctx.enter_context(tc.psum_pool(name="ps", bufs=1))
 
         list_a = sb.tile([P, J // 16], U16, name="list_a")
@@ -37,11 +40,11 @@ def tile_list_meet_plain_timestable_summed_kernel(
         list_f = sb.tile([P, I // 16], U16, name="list_f")
         x_words = sb.tile([P, T], I32, name="x_words", align_bytes=64)
         x_scales = sb.tile([P, T], U8, name="x_scales", align_bytes=64)
-        wa_raw = sb.tile([P, R], I32, name="wa_raw", align_bytes=64)
-        wa_raw_scales = sb.tile([P, R], U8, name="wa_raw_scales", tag="wa_scales_then_hb", align_bytes=64)
+        wa_raw = reused.tile([P, R], I32, name="wa_raw", align_bytes=64, offset=WA_AT + R)
+        wa_raw_scales = reused.tile([P, R], U8, name="wa_raw_scales", align_bytes=64, offset=WA_AT)
         wb_raw = sb.tile([P, R], U16, name="wb_raw", align_bytes=64)
         wb_raw_scales = sb.tile([P, R], U8, name="wb_raw_scales", align_bytes=64)
-        tf_rows = sb.tile([P, PACK * C], F32, name="tf_rows", tag="tf_then_ha", align_bytes=64)
+        tf_rows = reused.tile([P, PACK * C], F32, name="tf_rows", align_bytes=64, offset=TF_AT)
         cw_runs = sb.tile([P, 8], F32, name="cw_runs", align_bytes=64)
 
         for plane in (wb_raw_scales, wa_raw_scales):
@@ -121,14 +124,17 @@ def tile_list_meet_plain_timestable_summed_kernel(
         nc.vector.transpose(
             out=cw_turned[:].rearrange("p e n -> p (e n)"), in_=cw_wide[:].rearrange("p e n -> p (e n)")
         )
-        cw = sb.tile([P, 32, 8], F32, name="cw", align_bytes=64)
+        cw = reused.tile([P, 32, 8], F32, name="cw", align_bytes=64, offset=TF_AT + 2 * J * PACK)
         nc.scalar.activation(out=cw[:], in_=cw_turned[:].rearrange("p e n -> p n e"), func=ACT.Copy)
 
-        tf_picked = sb.tile([P, PACK, I], F32, name="tf_picked", align_bytes=64)
-        for t in range(PACK):
-            nc.scalar.activation(
-                out=tf_picked[:, t, :], in_=tf_rows[:, C * t : C * (t + 1)].indirect(list_f[:]), func=ACT.Copy
-            )
+        tf_picked = [sb.tile([P, PACK, HALF], F32, name="tf_picked%d" % h, align_bytes=64) for h in range(2)]
+        for h in range(2):
+            for t in range(PACK):
+                nc.scalar.activation(
+                    out=tf_picked[h][:, t, :],
+                    in_=tf_rows[:, C * t : C * (t + 1)].indirect(list_f[:, 8 * h : 8 * (h + 1)]),
+                    func=ACT.Copy,
+                )
 
         xb_words, xb_scales = gather_tokens("xb", list_b)
         xa_words, xa_scales = gather_tokens("xa", list_a)
@@ -140,13 +146,13 @@ def tile_list_meet_plain_timestable_summed_kernel(
         wa_dealt_scales = deal("wa_dealt_scales", wa_raw_scales, U8, 16)
         za = first_product("za", wa_dealt, E4M3, wa_dealt_scales, xa_words, xa_scales)
 
-        hb = sb.tile([P, I, PACK], BF16, name="hb", tag="wa_scales_then_hb", align_bytes=64)
+        hb = reused.tile([P, I, PACK], BF16, name="hb", align_bytes=64, offset=WA_AT)
         for h in range(2):
             cols = slice(HALF * h, HALF * (h + 1))
             nc.vector.tensor_tensor(
-                out=hb[:, cols, :],
-                in0=zb[h][:].rearrange("p t n -> p n t"),
-                in1=tf_picked[:, :, cols].rearrange("p t n -> p n t"),
+                out=hb[:, cols, :].rearrange("p (c i) t -> p c t i", i=4),
+                in0=zb[h][:].rearrange("p t (c i) -> p c t i", i=4),
+                in1=tf_picked[h][:].rearrange("p t (c i) -> p c t i", i=4),
                 op=MULT,
             )
         hb_words = sb.tile([P, I], U32, name="hb_words", align_bytes=64)
@@ -155,7 +161,7 @@ def tile_list_meet_plain_timestable_summed_kernel(
             out=hb_words[:].bitcast(E4M3), scales=hb_scales[:], in_=hb[:].rearrange("p n t -> p (n t)")
         )
 
-        ha = sb.tile([P, J * PACK], BF16, name="ha", tag="tf_then_ha", align_bytes=64)
+        ha = reused.tile([P, J * PACK], BF16, name="ha", align_bytes=64, offset=TF_AT)
         weighted = []
         for h in range(2):
             ha_half = ha[:, HALF * PACK * h : HALF * PACK * (h + 1)]

from contextlib import ExitStack

import concourse.mybir as mybir

K, T, J, I, R, C, S = 512, 512, 256, 256, 512, 512, 64
FLOPS = 2 * K * R * J + 2 * K * R * I + 2 * R * J * I

F32 = mybir.dt.float32
BF16 = mybir.dt.bfloat16
I32 = mybir.dt.int32
U32 = mybir.dt.uint32
U16 = mybir.dt.uint16
U8 = mybir.dt.uint8
E4M3 = mybir.dt.float8_e4m3fn_x4
E5M2 = mybir.dt.float8_e5m2_x4
E2M1 = mybir.dt.float4_e2m1fn_x4
MULT = mybir.AluOpType.mult
ADD = mybir.AluOpType.add
ACT = mybir.ActivationFunctionType

P = 128
PACK = 4
HALF = 128
OUT_SCALE = 0.04
TF_AT = 0
WA_AT = 4 * PACK * C


def tile_list_meet_plain_timestable_summed_kernel(
    tc, xt_words, xt_scales, wa_words, wa_scales, wb_words, wb_scales, tf, cw1, offs, offs2, offs3, out
):
    nc = tc.nc
    with ExitStack() as ctx:
        sb = ctx.enter_context(tc.tile_pool(name="sb", bufs=1))
        reused = ctx.enter_context(tc.tile_pool(name="reused", bufs=1))
        ps = ctx.enter_context(tc.psum_pool(name="ps", bufs=1))

        list_a = sb.tile([P, J // 16], U16, name="list_a")
        list_b = sb.tile([P, I // 16], U16, name="list_b")
        list_f = sb.tile([P, I // 16], U16, name="list_f")
        x_words = sb.tile([P, T], I32, name="x_words", align_bytes=64)
        x_scales = sb.tile([P, T], U8, name="x_scales", align_bytes=64)
        wa_raw = reused.tile([P, R], I32, name="wa_raw", align_bytes=64, offset=WA_AT + R)
        wa_raw_scales = reused.tile([P, R], U8, name="wa_raw_scales", align_bytes=64, offset=WA_AT)
        wb_raw = sb.tile([P, R], U16, name="wb_raw", align_bytes=64)
        wb_raw_scales = sb.tile([P, R], U8, name="wb_raw_scales", align_bytes=64)
        tf_rows = reused.tile([P, PACK * C], F32, name="tf_rows", align_bytes=64, offset=TF_AT)
        cw_runs = sb.tile([P, 8], F32, name="cw_runs", align_bytes=64)

        for plane in (wb_raw_scales, wa_raw_scales):
            nc.vector.memset(plane[:].bitcast(I32), 0)

        def load_scale_rows(queue, plane, rows, q):
            queue.dma_start(
                out=plane[32 * q : 32 * q + 4, :].bitcast(I32),
                in_=rows[0, 4 * q : 4 * q + 4, :].bitcast(I32),
            )

        def fill_scale_quadrant(queue, plane, rows, q):
            quad = rows[0, 4 * q : 4 * q + 4, :].bitcast(I32)
            queue.dma_start(
                out=plane[32 * q : 32 * q + 32, :].bitcast(I32),
                in_=quad.unsqueeze(0).to_broadcast([8, 4, T // 4]),
            )

        nc.sync.dma_start(out=list_b[:], in_=offs2)
        nc.scalar.dma_start(out=x_words[:], in_=xt_words[0].rearrange("p n t -> p (n t)").bitcast(I32))
        nc.gpsimd.dma_start(out=tf_rows[:], in_=tf.rearrange("(p t) c -> p (t c)", t=PACK))
        fill_scale_quadrant(nc.sync, x_scales, xt_scales, 0)
        fill_scale_quadrant(nc.scalar, x_scales, xt_scales, 1)
        fill_scale_quadrant(nc.sync, x_scales, xt_scales, 2)
        fill_scale_quadrant(nc.scalar, x_scales, xt_scales, 3)
        nc.sync.dma_start(out=cw_runs[:], in_=cw1[0].rearrange("(n e) -> n e", e=8).unsqueeze(0).to_broadcast([4, 32, 8]))
        nc.sync.dma_start(out=list_a[:], in_=offs)
        nc.sync.dma_start(out=list_f[:], in_=offs3)
        nc.sync.dma_start(out=wb_raw[:].bitcast(I32), in_=wb_words[0].bitcast(I32))
        load_scale_rows(nc.sync, wb_raw_scales, wb_scales, 0)
        load_scale_rows(nc.sync, wb_raw_scales, wb_scales, 1)
        load_scale_rows(nc.sync, wb_raw_scales, wb_scales, 2)
        load_scale_rows(nc.sync, wb_raw_scales, wb_scales, 3)
        nc.sync.dma_start(out=wa_raw[:], in_=wa_words[0].rearrange("p n t -> p (n t)").bitcast(I32))
        load_scale_rows(nc.sync, wa_raw_scales, wa_scales, 0)
        load_scale_rows(nc.gpsimd, wa_raw_scales, wa_scales, 1)
        load_scale_rows(nc.gpsimd, wa_raw_scales, wa_scales, 2)
        load_scale_rows(nc.gpsimd, wa_raw_scales, wa_scales, 3)

        def gather_tokens(name, offsets):
            words = sb.tile([P, J], U32, name=name + "_words", align_bytes=64)
            scales = sb.tile([P, J], U8, name=name + "_scales", align_bytes=64)
            nc.vector.tensor_copy(out=words[:], in_=x_words[:].bitcast(U32).indirect(offsets[:]))
            nc.vector.tensor_copy(out=scales[:], in_=x_scales[:].indirect(offsets[:]))
            return words, scales

        def deal(name, raw, dtype, line):
            dealt = sb.tile([P, R], dtype, name=name, align_bytes=64)
            nc.vector.tensor_copy(
                out=dealt[:].rearrange("p (t c i) -> p c t i", t=PACK, i=line),
                in_=raw[:].rearrange("p (c i t) -> p c t i", t=PACK, i=line),
            )
            return dealt

        def first_product(name, w_words, w_format, w_scales, words, scales):
            banks = []
            for h in range(2):
                bank = ps.tile([P, PACK, HALF], F32, name="%s%d" % (name, h))
                cols = slice(HALF * h, HALF * (h + 1))
                for t in range(PACK):
                    rows = slice(P * t, P * (t + 1))
                    nc.tensor.matmul_mx(
                        out=bank[:, t, :],
                        lhsT=w_words[:, rows].bitcast(w_format),
                        lhsT_scale=w_scales[:, rows],
                        rhs=words[:, cols].bitcast(E5M2),
                        rhs_scale=scales[:, cols],
                        start=True,
                        stop=True,
                    )
                banks.append(bank)
            return banks

        cw_wide = sb.tile([P, 8, 32], F32, name="cw_wide", align_bytes=64)
        nc.scalar.activation(out=cw_wide[:], in_=cw_runs[:].unsqueeze(2).to_broadcast([P, 8, 32]), func=ACT.Copy)
        cw_turned = sb.tile([P, 8, 32], F32, name="cw_turned", align_bytes=64)
        nc.vector.transpose(
            out=cw_turned[:].rearrange("p e n -> p (e n)"), in_=cw_wide[:].rearrange("p e n -> p (e n)")
        )
        cw = reused.tile([P, 32, 8], F32, name="cw", align_bytes=64, offset=TF_AT + 2 * J * PACK)
        nc.scalar.activation(out=cw[:], in_=cw_turned[:].rearrange("p e n -> p n e"), func=ACT.Copy)

        tf_picked = [sb.tile([P, PACK, HALF], F32, name="tf_picked%d" % h, align_bytes=64) for h in range(2)]
        for h in range(2):
            for t in range(PACK):
                nc.scalar.activation(
                    out=tf_picked[h][:, t, :],
                    in_=tf_rows[:, C * t : C * (t + 1)].indirect(list_f[:, 8 * h : 8 * (h + 1)]),
                    func=ACT.Copy,
                )

        xb_words, xb_scales = gather_tokens("xb", list_b)
        xa_words, xa_scales = gather_tokens("xa", list_a)
        wb_dealt = deal("wb_dealt", wb_raw, U16, 8)
        wb_dealt_scales = deal("wb_dealt_scales", wb_raw_scales, U8, 16)
        zb = first_product("zb", wb_dealt, E2M1, wb_dealt_scales, xb_words, xb_scales)

        wa_dealt = deal("wa_dealt", wa_raw, I32, 4)
        wa_dealt_scales = deal("wa_dealt_scales", wa_raw_scales, U8, 16)
        za = first_product("za", wa_dealt, E4M3, wa_dealt_scales, xa_words, xa_scales)

        hb = reused.tile([P, I, PACK], BF16, name="hb", align_bytes=64, offset=WA_AT)
        for h in range(2):
            cols = slice(HALF * h, HALF * (h + 1))
            nc.vector.tensor_tensor(
                out=hb[:, cols, :].rearrange("p (c i) t -> p c t i", i=4),
                in0=zb[h][:].rearrange("p t (c i) -> p c t i", i=4),
                in1=tf_picked[h][:].rearrange("p t (c i) -> p c t i", i=4),
                op=MULT,
            )
        hb_words = sb.tile([P, I], U32, name="hb_words", align_bytes=64)
        hb_scales = sb.tile([P, I], U8, name="hb_scales", align_bytes=64)
        nc.vector.quantize_mx(
            out=hb_words[:].bitcast(E4M3), scales=hb_scales[:], in_=hb[:].rearrange("p n t -> p (n t)")
        )

        ha = reused.tile([P, J * PACK], BF16, name="ha", align_bytes=64, offset=TF_AT)
        weighted = []
        for h in range(2):
            ha_half = ha[:, HALF * PACK * h : HALF * PACK * (h + 1)]
            nc.scalar.activation(
                out=ha_half.rearrange("p (n t) -> p n t", t=PACK),
                in_=za[h][:].rearrange("p t n -> p n t"),
                func=ACT.Relu,
            )
            ha_words = sb.tile([P, HALF], U32, name="ha_words%d" % h, align_bytes=64)
            ha_scales = sb.tile([P, HALF], U8, name="ha_scales%d" % h, align_bytes=64)
            nc.vector.quantize_mx(out=ha_words[:].bitcast(E5M2), scales=ha_scales[:], in_=ha_half)
            scores = ps.tile([P, I], F32, name="scores%d" % h)
            nc.tensor.matmul_mx(
                out=scores[:],
                lhsT=ha_words[:].bitcast(E5M2),
                lhsT_scale=ha_scales[:],
                rhs=hb_words[:].bitcast(E4M3),
                rhs_scale=hb_scales[:],
                start=True,
                stop=True,
            )
            product = sb.tile([P, S, I // S], F32, name="weighted%d" % h, align_bytes=64)
            weighted.append((scores, product))

        for scores, product in weighted:
            nc.vector.scalar_tensor_tensor(
                out=product[:].rearrange("p s u -> p (s u)"),
                in0=scores[:],
                scalar=OUT_SCALE,
                in1=cw[:].rearrange("p n e -> p (n e)"),
                op0=MULT,
                op1=MULT,
            )
        for h, (scores, product) in enumerate(weighted):
            summed = sb.tile([P, S], F32, name="summed%d" % h, align_bytes=64)
            nc.vector.tensor_reduce(out=summed[:], in_=product[:], axis=mybir.AxisListType.X, op=ADD)
            (nc.sync, nc.scalar)[h].dma_start(out=out[HALF * h : HALF * (h + 1), :], in_=summed[:])
